import numpy as np
import ml_dtypes


def mxq(x, axis, fmt="e4m3"):
    dtype, down = {"e4m3": (ml_dtypes.float8_e4m3fn, 7), "e5m2": (ml_dtypes.float8_e5m2, 14)}[fmt]
    v = np.moveaxis(np.asarray(x, np.float32).astype(ml_dtypes.bfloat16).astype(np.float64), axis, -1)
    blocks = v.reshape(v.shape[:-1] + (-1, 32))
    amax = np.abs(blocks).max(-1, keepdims=True)
    byte = np.maximum(np.where(amax > 0, np.frexp(amax)[1] - 1 + 127, 0) - down, 1)
    scale = np.exp2(byte - 127.0)
    codes = (blocks / scale).astype(np.float32).astype(dtype).astype(np.float64)
    return np.moveaxis((codes * scale).reshape(v.shape), -1, axis)


WIDE = False


def mx_kscale(k):
    if not WIDE:
        return np.ones(k)
    levels = np.array([10, -10, 5, -5, 0])
    if k % 512:
        return np.exp2(np.random.permutation(np.resize(levels, k // 32))).repeat(32)
    a = np.empty((k // 512, 16))
    for p in range(k // 512):
        a[p, :8] = np.random.permutation(np.resize(levels, 8))
        for g in range(8):
            far = levels[np.abs(levels - a[p, g]) >= 10]
            a[p, g + 8] = far[np.random.randint(len(far))]
    return np.exp2(a.ravel()).repeat(32)


BF16 = ml_dtypes.bfloat16


def bf(x):
    return np.asarray(x, np.float32).astype(BF16)


def f64(x):
    return np.asarray(x).astype(np.float64)


E2M1 = np.array([0.0, 0.5, 1.0, 1.5, 2.0, 3.0, 4.0, 6.0, -0.0, -0.5, -1.0, -1.5, -2.0, -3.0, -4.0, -6.0])


def pack_weight(w, fmt):
    k, n = w.shape
    w = f64(bf(w)).reshape(k // 32, 32, n)
    amax = np.abs(w).max(1)
    if fmt == "e4m3":
        byte = np.frexp(amax)[1] - 1 + 127 - 7
    else:
        mant, ex = np.frexp(amax / 6.0)
        byte = np.where(mant > 0.5, ex, ex - 1) + 127
    byte = np.clip(np.where(amax > 0, byte, 1), 1, 254)
    scaled = (w * np.exp2(127.0 - byte)[:, None, :]).reshape(k, n).astype(np.float32)
    by_word = np.ascontiguousarray(scaled.reshape(k // 512, 128, 4, n).transpose(0, 1, 3, 2))
    if fmt == "e4m3":
        words = by_word.astype(ml_dtypes.float8_e4m3fn).view(np.uint8)
    else:
        c = by_word.astype(ml_dtypes.float4_e2m1fn).view(np.uint8) & 0xF
        words = c[..., 0::2] | (c[..., 1::2] << 4)
    return np.ascontiguousarray(words), np.ascontiguousarray(byte.astype(np.uint8).reshape(k // 512, 16, n))


def unpack_weight(words, scales, fmt):
    g, p, n, _ = words.shape
    if fmt == "e4m3":
        vals = np.ascontiguousarray(words).view(ml_dtypes.float8_e4m3fn).astype(np.float64)
    else:
        nib = np.empty((g, p, n, 4), np.uint8)
        nib[..., 0::2] = words & 0xF
        nib[..., 1::2] = words >> 4
        vals = E2M1[nib]
    vals = vals * np.repeat(np.exp2(scales.astype(np.float64) - 127.0), 8, axis=1)[..., None]
    return vals.transpose(0, 1, 3, 2).reshape(g * 512, n)

def planes(Y):
    n, m = Y.shape
    b = f64(bf(Y)).reshape(n // 32, 32, m)
    amax = np.abs(b).max(1)
    byte = np.clip(np.where(amax > 0, np.frexp(amax)[1] - 1 + 127 - 7, 1), 1, 254)
    codes = (b * np.exp2(127.0 - byte)[:, None, :]).reshape(n, m).astype(np.float32).astype(ml_dtypes.float8_e4m3fn).view(np.uint8)
    words = codes.reshape(n // 512, 128, 4, m).transpose(0, 1, 3, 2)
    return np.ascontiguousarray(words), np.ascontiguousarray(byte.astype(np.uint8).reshape(n // 512, 16, m))


T, N, R, O = 1024, 1024, 512, 512


def setup_inputs():
    s, t = mx_kscale(N), mx_kscale(R)
    x = bf(np.random.standard_normal((T, N)) * s)
    a_words, a_scales = pack_weight(np.random.standard_normal((N, R)) / np.sqrt(N) / s[:, None], "e4m3")
    b_words, b_scales = pack_weight(np.random.standard_normal((N, R)) / np.sqrt(N) / s[:, None] * t, "e4m3")
    h1_words, h1_scales = pack_weight(np.random.standard_normal((N, O)) / np.sqrt(N) / s[:, None], "e4m3")
    h2_words, h2_scales = pack_weight(np.random.standard_normal((R, O)) / np.sqrt(R) / t[:, None], "e4m3")
    h3_words, h3_scales = pack_weight(0.5 * np.random.standard_normal((R, O)) / np.sqrt(R) / t[:, None], "e4m3")
    return {
        "x": x,
        "a_words": a_words,
        "a_scales": a_scales,
        "b_words": b_words,
        "b_scales": b_scales,
        "h1_words": h1_words,
        "h1_scales": h1_scales,
        "h2_words": h2_words,
        "h2_scales": h2_scales,
        "h3_words": h3_words,
        "h3_scales": h3_scales,
    }


def core(x, a_words, a_scales, b_words, b_scales, h1_words, h1_scales, h2_words, h2_scales, h3_words, h3_scales):
    xq = mxq(f64(x), 1, "e4m3")
    p = xq @ unpack_weight(a_words, a_scales, "e4m3")
    q = xq @ unpack_weight(b_words, b_scales, "e4m3")
    k2 = p * q
    k3 = p * k2
    y1 = xq @ unpack_weight(h1_words, h1_scales, "e4m3")
    y2 = mxq(k2, 1, "e4m3") @ unpack_weight(h2_words, h2_scales, "e4m3")
    y3 = mxq(k3, 1, "e4m3") @ unpack_weight(h3_words, h3_scales, "e4m3")
    return y1 + y2 + y3


def reference(x, a_words, a_scales, b_words, b_scales, h1_words, h1_scales, h2_words, h2_scales, h3_words, h3_scales):
    R_out = core(x, a_words, a_scales, b_words, b_scales, h1_words, h1_scales, h2_words, h2_scales, h3_words, h3_scales)
    words, scales = planes(R_out)
    return R_out, words, scales

@@ -1,0 +1,387 @@
+from contextlib import ExitStack
+
+import concourse.mybir as mybir
+from concourse.masks import make_identity
+
+F32 = mybir.dt.float32
+BF16 = mybir.dt.bfloat16
+I32 = mybir.dt.int32
+U8 = mybir.dt.uint8
+FP8X4 = mybir.dt.float8_e4m3fn_x4
+MULT = mybir.AluOpType.mult
+
+T, N, R, O = 1024, 1024, 512, 512
+FLOPS = 2 * T * (N * R * 2 + N * O + R * O * 2)
+P = 128
+PACK = 4
+KP = 512
+
+
+def tile_factoredcubicvolterraequalizer_x2_kernel(
+    tc, x, a_words, a_scales, b_words, b_scales, h1_words, h1_scales,
+    h2_words, h2_scales, h3_words, h3_scales, out_0, out_1, out_2,
+):
+    nc = tc.nc
+    with ExitStack() as ctx:
+        keep = ctx.enter_context(tc.tile_pool(name="keep", bufs=1))
+        work = ctx.enter_context(tc.tile_pool(name="work", bufs=3))
+        psum = ctx.enter_context(tc.psum_pool(name="psum", bufs=8))
+        ctx.enter_context(tc.manual_schedule())
+
+        ident = keep.tile([P, P], F32, align_bytes=64)
+        ab_raw_pl = keep.tile([P, 512], U8, align_bytes=64)
+        ab_pl = keep.tile([P, 512], U8, align_bytes=64)
+        h_pl = keep.tile([P, 512], U8, align_bytes=64)
+        a_raw = keep.tile([P, 2, 512], I32, align_bytes=64)
+        b_raw = keep.tile([P, 2, 512], I32, align_bytes=64)
+        a_cod = keep.tile([P, 2, 512], I32, align_bytes=64)
+        b_cod = keep.tile([P, 2, 512], I32, align_bytes=64)
+        h_cod = keep.tile([P, 4, 512], I32, align_bytes=64)
+        x_raw = []
+        for c in range(2):
+            x_one = keep.tile([P, 1, N], BF16, align_bytes=64, name="x_one%d" % c)
+            x_raw.append((x_one, 0))
+        for c in range(2, 8, 2):
+            x_two = keep.tile([P, 2, N], BF16, align_bytes=64, name="x_two%d" % c)
+            x_raw.extend([(x_two, 0), (x_two, 1)])
+        x_cod = [keep.tile([P, 256], I32, align_bytes=64, name="x_cod%d" % c) for c in range(8)]
+        x_pl = [keep.tile([P, 256], U8, align_bytes=64, name="x_pl%d" % c) for c in range(8)]
+        k_cod = [keep.tile([P, 256], I32, align_bytes=64, name="k_cod%d" % c) for c in range(8)]
+        k_pl = [keep.tile([P, 256], U8, align_bytes=64, name="k_pl%d" % c) for c in range(8)]
+        y_sb = [keep.tile([P, 4, 512], F32, align_bytes=64, name="y_sb%d" % g) for g in range(2)]
+        y_cod = [keep.tile([P, 512], I32, align_bytes=64, name="y_cod%d" % g) for g in range(2)]
+        y_pl = [keep.tile([P, 512], U8, align_bytes=64, name="y_pl%d" % g) for g in range(2)]
+
+        x_v = [x[512 * g : 512 * g + 512, :].rearrange("(p t) k -> p t k", t=4) for g in range(2)]
+        o_v = [out_0[512 * g : 512 * g + 512, :].rearrange("(p t) m -> p t m", t=4) for g in range(2)]
+
+        nc.vector.memset(ab_raw_pl[:].bitcast(I32), 0)
+        nc.vector.memset(h_pl[:].bitcast(I32), 0)
+        make_identity(nc, ident[:])
+
+        def load_x(c, count):
+            nc.sync.dma_start(out=x_raw[c][0][:], in_=x_v[c // 4][:, c % 4 : c % 4 + count, :])
+
+        def load_w(tile_ap, words):
+            nc.sync.dma_start(out=tile_ap, in_=words.rearrange("g p n t -> p g (n t)").bitcast(I32))
+
+        def load_s(eng, plane, row, scales):
+            passes = scales.shape[0]
+            for q in range(4):
+                r0 = 32 * q + row
+                eng.dma_start(
+                    out=plane[r0 : r0 + 4 * passes, :].bitcast(I32),
+                    in_=scales[:, 4 * q : 4 * q + 4, :].bitcast(I32),
+                )
+
+        load_x(0, 1)
+        load_s(nc.scalar, ab_raw_pl, 0, a_scales)
+        load_w(a_raw[:], a_words)
+        load_x(1, 1)
+        load_w(b_raw[:], b_words)
+        load_s(nc.sync, ab_raw_pl, 8, b_scales)
+        load_x(2, 2)
+        load_w(h_cod[:, 0:2, :], h1_words)
+        load_x(4, 2)
+        load_w(h_cod[:, 2:3, :], h2_words)
+        load_w(h_cod[:, 3:4, :], h3_words)
+        load_x(6, 2)
+        load_s(nc.sync, h_pl, 0, h1_scales)
+        load_s(nc.sync, h_pl, 8, h2_scales)
+        load_s(nc.sync, h_pl, 12, h3_scales)
+
+        def bank(nm):
+            return psum.tile([P, 512], F32, tag="bank", name=nm)
+
+        xt, xb, pb, qb, psb, k2f, kb = {}, {}, {}, {}, {}, {}, {}
+
+        def transpose_x(c):
+            xt[c] = bank("xt")
+            words = x_raw[c][0][:, x_raw[c][1], :].bitcast(F32)
+            for g in range(2):
+                for u in range(2):
+                    col = (2 * g + u) * P
+                    nc.tensor.transpose(
+                        xt[c][:, col : col + P], words[:, 256 * g + u : 256 * (g + 1) : 2], ident[:]
+                    )
+
+        def copy_x(c):
+            xb[c] = work.tile([P, N], BF16, align_bytes=64, tag="xb", name="xb")
+            nc.scalar.copy(
+                out=xb[c][:].bitcast(F32).rearrange("p (g r u) -> p g r u", g=2, u=2),
+                in_=xt[c][:].rearrange("p (g u r) -> p g r u", g=2, u=2),
+            )
+
+        def quant_x(c):
+            nc.vector.quantize_mx(out=x_cod[c][:].bitcast(FP8X4), scales=x_pl[c][:], in_=xb[c][:])
+
+        def perm(cod, raw):
+            nc.vector.tensor_copy(
+                out=cod[:].rearrange("p g (t m) -> p g t m", t=4),
+                in_=raw[:].rearrange("p g (m t) -> p g t m", t=4),
+            )
+
+        def perm_scales():
+            nc.vector.tensor_copy(
+                out=ab_pl[:].rearrange("p (t m) -> p t m", t=4),
+                in_=ab_raw_pl[:].rearrange("p (m t) -> p t m", t=4),
+            )
+
+        def stage1(c, cod, row, banks, nm):
+            banks[c] = bank(nm)
+            for t in range(4):
+                for g in range(2):
+                    nc.tensor.matmul_mx(
+                        out=banks[c][:, t * P : (t + 1) * P],
+                        lhsT=cod[:, g, t * P : (t + 1) * P].bitcast(FP8X4),
+                        lhsT_scale=ab_pl[row + 4 * g : P, t * P : (t + 1) * P],
+                        rhs=x_cod[c][:, g * P : (g + 1) * P].bitcast(FP8X4),
+                        rhs_scale=x_pl[c][:, g * P : (g + 1) * P],
+                        start=(g == 0),
+                        stop=(g == 1),
+                    )
+
+        def copy_p(c):
+            psb[c] = work.tile([P, 512], F32, align_bytes=64, tag="psb", name="psb")
+            nc.scalar.copy(
+                out=psb[c][:].rearrange("p (n t) -> p n t", t=4),
+                in_=pb[c][:].rearrange("p (t n) -> p n t", t=4),
+            )
+
+        def make_k2(c):
+            k2f[c] = work.tile([P, 512], F32, align_bytes=64, tag="k2f", name="k2f")
+            nc.vector.tensor_tensor(
+                out=k2f[c][:].rearrange("p (n t) -> p n t", t=4),
+                in0=qb[c][:].rearrange("p (t n) -> p n t", t=4),
+                in1=psb[c][:].rearrange("p (n t) -> p n t", t=4),
+                op=MULT,
+            )
+            kb[c] = work.tile([P, 1024], BF16, align_bytes=64, tag="kb", name="kb")
+
+        def make_k3(c):
+            nc.vector.tensor_tensor(out=kb[c][:, 512:1024], in0=k2f[c][:], in1=psb[c][:], op=MULT)
+
+        def cast_k2(c):
+            nc.scalar.copy(out=kb[c][:, 0:512], in_=k2f[c][:])
+
+        def quant_k(c):
+            nc.vector.quantize_mx(out=k_cod[c][:].bitcast(FP8X4), scales=k_pl[c][:], in_=kb[c][:])
+
+
+        stage2_operands = [(x_cod, x_pl, 0, 0), (x_cod, x_pl, 1, 1), (k_cod, k_pl, 0, 2), (k_cod, k_pl, 1, 3)]
+
+        def stage2(c, out_ap, m0, width, passes):
+            for i in passes:
+                cod, pl, half, h = stage2_operands[i]
+                nc.tensor.matmul_mx(
+                    out=out_ap,
+                    lhsT=cod[c][:, half * P : (half + 1) * P].bitcast(FP8X4),
+                    lhsT_scale=pl[c][:, half * P : (half + 1) * P],
+                    rhs=h_cod[:, h, m0 : m0 + width].bitcast(FP8X4),
+                    rhs_scale=h_pl[4 * h : P, m0 : m0 + width],
+                    start=(i == 0),
+                    stop=(i == 3),
+                )
+
+        ybank, yb = {}, {}
+
+        def stage2_wide(c):
+            ybank[c] = bank("ybank")
+            stage2(c, ybank[c][:], 0, 512, range(4))
+
+        def copy_y(c):
+            g, t = divmod(c, 4)
+            nc.scalar.copy(out=y_sb[g][:, t, :], in_=ybank[c][:])
+
+        def store_y(c):
+            g, t = divmod(c, 4)
+            nc.sync.dma_start(out=o_v[g][:, t, :], in_=y_sb[g][:, t, :])
+
+        last = {}
+
+        def last_x(q):
+            last[q] = bank("last")
+            stage2(7, last[q][:, :P], q * P, P, range(2))
+
+        def last_k(q):
+            stage2(7, last[q][:, :P], q * P, P, range(2, 4))
+
+        def copy_last(q):
+            nc.scalar.copy(out=y_sb[1][:, 3, q * P : (q + 1) * P], in_=last[q][:, :P])
+
+        def copy_last_v(q):
+            nc.vector.tensor_copy(out=y_sb[1][:, 3, q * P : (q + 1) * P], in_=last[q][:, :P])
+
+        def store_y_last():
+            nc.sync.dma_start(out=o_v[1][:, 3, :], in_=y_sb[1][:, 3, :])
+
+        def cast_k2_v(c):
+            nc.vector.tensor_copy(out=kb[c][:, 0:512], in_=k2f[c][:])
+
+        def interleave_y(g, m0, width, engine):
+            yb[g, m0] = work.tile([P, 1024], BF16, align_bytes=64, tag="yb", name="yb")
+            copy = nc.scalar.copy if engine == "scalar" else nc.vector.tensor_copy
+            copy(
+                out=yb[g, m0][:, : 4 * width].rearrange("p (m t) -> p m t", t=4),
+                in_=y_sb[g][:, :, m0 : m0 + width].rearrange("p t m -> p m t"),
+            )
+
+        def quant_y(g, m0, width):
+            nc.vector.quantize_mx(
+                out=y_cod[g][:, m0 : m0 + width].bitcast(FP8X4),
+                scales=y_pl[g][:, m0 : m0 + width],
+                in_=yb[g, m0][:, : 4 * width],
+            )
+
+        def store_codes(g, m0, width):
+            nc.sync.dma_start(
+                out=out_1[g].rearrange("p m t -> p (m t)")[:, 4 * m0 : 4 * (m0 + width)].bitcast(I32),
+                in_=y_cod[g][:, m0 : m0 + width],
+            )
+
+        def store_scales(g):
+            for q in range(4):
+                nc.sync.dma_start(
+                    out=out_2[g, 4 * q : 4 * q + 4, :].bitcast(I32), in_=y_pl[g][32 * q : 32 * q + 4, :].bitcast(I32)
+                )
+
+        def p_of(c):
+            stage1(c, a_cod, 0, pb, "pb")
+
+        def q_of(c):
+            stage1(c, b_cod, 8, qb, "qb")
+
+        transpose_x(0)
+        copy_x(0)
+        perm(a_cod, a_raw)
+        transpose_x(1)
+        copy_x(1)
+        quant_x(0)
+        perm_scales()
+        p_of(0)
+        copy_p(0)
+        quant_x(1)
+        transpose_x(2)
+        copy_x(2)
+        perm(b_cod, b_raw)
+        transpose_x(3)
+        copy_x(3)
+        quant_x(2)
+        p_of(1)
+        copy_p(1)
+        quant_x(3)
+        q_of(0)
+        make_k2(0)
+        q_of(1)
+        cast_k2(0)
+        make_k3(0)
+        p_of(2)
+        copy_p(2)
+        make_k2(1)
+        q_of(2)
+        cast_k2(1)
+        quant_k(0)
+        transpose_x(4)
+        copy_x(4)
+        make_k3(1)
+        transpose_x(5)
+        copy_x(5)
+        quant_k(1)
+        p_of(3)
+        copy_p(3)
+        make_k2(2)
+        q_of(3)
+        cast_k2(2)
+        quant_x(4)
+        stage2_wide(0)
+        copy_y(0)
+        make_k3(2)
+        store_y(0)
+        p_of(4)
+        copy_p(4)
+        quant_x(5)
+        q_of(4)
+        quant_k(2)
+        transpose_x(6)
+        make_k2(3)
+        transpose_x(7)
+        cast_k2(3)
+        make_k3(3)
+        stage2_wide(1)
+        copy_x(6)
+        quant_k(3)
+        p_of(5)
+        copy_x(7)
+        make_k2(4)
+        q_of(5)
+        copy_y(1)
+        quant_x(6)
+        store_y(1)
+        stage2_wide(2)
+        copy_p(5)
+        make_k3(4)
+        p_of(6)
+        cast_k2(4)
+        quant_x(7)
+        q_of(6)
+        copy_y(2)
+        quant_k(4)
+        store_y(2)
+        stage2_wide(3)
+        copy_p(6)
+        make_k2(5)
+        p_of(7)
+        cast_k2(5)
+        make_k3(5)
+        q_of(7)
+        copy_y(3)
+        quant_k(5)
+        store_y(3)
+        stage2_wide(4)
+        copy_p(7)
+        make_k2(6)
+        stage2_wide(5)
+        cast_k2(6)
+        make_k3(6)
+        copy_y(4)
+        quant_k(6)
+        store_y(4)
+        stage2_wide(6)
+        make_k2(7)
+        last_x(0)
+        cast_k2(7)
+        interleave_y(0, 0, 256, "vector")
+        last_x(1)
+        copy_y(5)
+        make_k3(7)
+        store_y(5)
+        last_x(2)
+        copy_y(6)
+        quant_y(0, 0, 256)
+        store_y(6)
+        last_x(3)
+        quant_k(7)
+        last_k(0)
+        copy_last(0)
+        interleave_y(0, 256, 256, "vector")
+        last_k(1)
+        copy_last(1)
+        quant_y(0, 256, 256)
+        store_codes(0, 0, 512)
+        last_k(2)
+        copy_last(2)
+        interleave_y(1, 0, 128, "vector")
+        store_scales(0)
+        last_k(3)
+        copy_last(3)
+        interleave_y(1, 128, 128, "vector")
+        store_y_last()
+        interleave_y(1, 384, 128, "scalar")
+        quant_y(1, 0, 128)
+        interleave_y(1, 256, 128, "vector")
+        quant_y(1, 128, 128)
+        store_codes(1, 0, 256)
+        quant_y(1, 256, 128)
+        quant_y(1, 384, 128)
+        store_codes(1, 256, 256)
+        store_scales(1)

@@ -24,13 +24,13 @@ def tile_factoredcubicvolterraequalizer_x2_kernel(
     nc = tc.nc
     with ExitStack() as ctx:
         keep = ctx.enter_context(tc.tile_pool(name="keep", bufs=1))
-        work = ctx.enter_context(tc.tile_pool(name="work", bufs=3))
+        work = ctx.enter_context(tc.tile_pool(name="work", bufs=4))
         psum = ctx.enter_context(tc.psum_pool(name="psum", bufs=8))
         ctx.enter_context(tc.manual_schedule())
 
         ident = keep.tile([P, P], F32, align_bytes=64)
-        ab_raw_pl = keep.tile([P, 512], U8, align_bytes=64)
-        ab_pl = keep.tile([P, 512], U8, align_bytes=64)
+        raw_pl = [keep.tile([P, 512], U8, align_bytes=64, name="raw_pl%d" % i) for i in range(2)]
+        perm_pl = [keep.tile([P, 512], U8, align_bytes=64, name="perm_pl%d" % i) for i in range(2)]
         h_pl = keep.tile([P, 512], U8, align_bytes=64)
         a_raw = keep.tile([P, 2, 512], I32, align_bytes=64)
         b_raw = keep.tile([P, 2, 512], I32, align_bytes=64)
@@ -55,37 +55,46 @@ def tile_factoredcubicvolterraequalizer_x2_kernel(
         x_v = [x[512 * g : 512 * g + 512, :].rearrange("(p t) k -> p t k", t=4) for g in range(2)]
         o_v = [out_0[512 * g : 512 * g + 512, :].rearrange("(p t) m -> p t m", t=4) for g in range(2)]
 
-        nc.vector.memset(ab_raw_pl[:].bitcast(I32), 0)
+        nc.vector.memset(raw_pl[0][:].bitcast(I32), 0)
+        zero = keep.tile([P, 512], BF16, align_bytes=64)
+        warm_cod = keep.tile([P, P], I32, align_bytes=64)
+        warm_pl = keep.tile([P, P], U8, align_bytes=64)
+        nc.vector.memset(zero[:].bitcast(I32), 0)
+        nc.vector.memset(raw_pl[1][:].bitcast(I32), 0)
+        nc.vector.quantize_mx(out=warm_cod[:].bitcast(FP8X4), scales=warm_pl[:], in_=zero[:])
         nc.vector.memset(h_pl[:].bitcast(I32), 0)
-        make_identity(nc, ident[:])
 
-        def load_x(c, count):
-            nc.sync.dma_start(out=x_raw[c][0][:], in_=x_v[c // 4][:, c % 4 : c % 4 + count, :])
+        def load_x(c, count, k0=0, k1=N):
+            nc.sync.dma_start(
+                out=x_raw[c][0][:, :, k0:k1], in_=x_v[c // 4][:, c % 4 : c % 4 + count, k0:k1]
+            )
 
-        def load_w(tile_ap, words):
-            nc.sync.dma_start(out=tile_ap, in_=words.rearrange("g p n t -> p g (n t)").bitcast(I32))
+        def load_w(eng, tile_ap, words):
+            eng.dma_start(out=tile_ap, in_=words.rearrange("g p n t -> p g (n t)").bitcast(I32))
 
-        def load_s(eng, plane, row, scales):
+        def load_s(eng, plane, row, scales, quadrants=range(4)):
             passes = scales.shape[0]
-            for q in range(4):
+            for q in quadrants:
                 r0 = 32 * q + row
                 eng.dma_start(
                     out=plane[r0 : r0 + 4 * passes, :].bitcast(I32),
                     in_=scales[:, 4 * q : 4 * q + 4, :].bitcast(I32),
                 )
 
-        load_x(0, 1)
-        load_s(nc.scalar, ab_raw_pl, 0, a_scales)
-        load_w(a_raw[:], a_words)
+        load_x(0, 1, 0, 512)
+        load_x(0, 1, 512, N)
+        load_s(nc.scalar, raw_pl[0], 0, a_scales)
+        load_w(nc.scalar, a_raw[:], a_words)
+        load_s(nc.sync, raw_pl[1], 0, b_scales)
+        load_w(nc.gpsimd, b_raw[:], b_words)
+        make_identity(nc, ident[:])
         load_x(1, 1)
-        load_w(b_raw[:], b_words)
-        load_s(nc.sync, ab_raw_pl, 8, b_scales)
         load_x(2, 2)
-        load_w(h_cod[:, 0:2, :], h1_words)
+        load_w(nc.sync, h_cod[:, 0:2, :], h1_words)
         load_x(4, 2)
-        load_w(h_cod[:, 2:3, :], h2_words)
-        load_w(h_cod[:, 3:4, :], h3_words)
         load_x(6, 2)
+        load_w(nc.sync, h_cod[:, 2:3, :], h2_words)
+        load_w(nc.sync, h_cod[:, 3:4, :], h3_words)
         load_s(nc.sync, h_pl, 0, h1_scales)
         load_s(nc.sync, h_pl, 8, h2_scales)
         load_s(nc.sync, h_pl, 12, h3_scales)
@@ -95,15 +104,24 @@ def tile_factoredcubicvolterraequalizer_x2_kernel(
 
         xt, xb, pb, qb, psb, k2f, kb = {}, {}, {}, {}, {}, {}, {}
 
-        def transpose_x(c):
-            xt[c] = bank("xt")
+        def transpose_x(c, groups=(0, 1)):
+            if 0 in groups:
+                xt[c] = bank("xt")
             words = x_raw[c][0][:, x_raw[c][1], :].bitcast(F32)
-            for g in range(2):
+            for g in groups:
                 for u in range(2):
                     col = (2 * g + u) * P
                     nc.tensor.transpose(
                         xt[c][:, col : col + P], words[:, 256 * g + u : 256 * (g + 1) : 2], ident[:]
                     )
+
+        def copy_x_half(c, g):
+            if g == 0:
+                xb[c] = work.tile([P, N], BF16, align_bytes=64, tag="xb", name="xb")
+            nc.scalar.copy(
+                out=xb[c][:, 512 * g : 512 * (g + 1)].bitcast(F32).rearrange("p (r u) -> p r u", u=2),
+                in_=xt[c][:, 256 * g : 256 * (g + 1)].rearrange("p (u r) -> p r u", u=2),
+            )
 
         def copy_x(c):
             xb[c] = work.tile([P, N], BF16, align_bytes=64, tag="xb", name="xb")
@@ -115,26 +133,26 @@ def tile_factoredcubicvolterraequalizer_x2_kernel(
         def quant_x(c):
             nc.vector.quantize_mx(out=x_cod[c][:].bitcast(FP8X4), scales=x_pl[c][:], in_=xb[c][:])
 
-        def perm(cod, raw):
+        def perm(cod, raw, t0, t1):
             nc.vector.tensor_copy(
-                out=cod[:].rearrange("p g (t m) -> p g t m", t=4),
-                in_=raw[:].rearrange("p g (m t) -> p g t m", t=4),
+                out=cod[:].rearrange("p g (t m) -> p g t m", t=4)[:, :, t0:t1, :],
+                in_=raw[:].rearrange("p g (m t) -> p g t m", t=4)[:, :, t0:t1, :],
             )
 
-        def perm_scales():
+        def perm_scales(i):
             nc.vector.tensor_copy(
-                out=ab_pl[:].rearrange("p (t m) -> p t m", t=4),
-                in_=ab_raw_pl[:].rearrange("p (m t) -> p t m", t=4),
+                out=perm_pl[i][:].rearrange("p (t m) -> p t m", t=4),
+                in_=raw_pl[i][:].rearrange("p (m t) -> p t m", t=4),
             )
 
-        def stage1(c, cod, row, banks, nm):
+        def stage1(c, cod, i, banks, nm):
             banks[c] = bank(nm)
             for t in range(4):
                 for g in range(2):
                     nc.tensor.matmul_mx(
                         out=banks[c][:, t * P : (t + 1) * P],
                         lhsT=cod[:, g, t * P : (t + 1) * P].bitcast(FP8X4),
-                        lhsT_scale=ab_pl[row + 4 * g : P, t * P : (t + 1) * P],
+                        lhsT_scale=perm_pl[i][4 * g : P, t * P : (t + 1) * P],
                         rhs=x_cod[c][:, g * P : (g + 1) * P].bitcast(FP8X4),
                         rhs_scale=x_pl[c][:, g * P : (g + 1) * P],
                         start=(g == 0),
@@ -199,21 +217,21 @@ def tile_factoredcubicvolterraequalizer_x2_kernel(
 
         last = {}
 
-        def last_x(q):
-            last[q] = bank("last")
-            stage2(7, last[q][:, :P], q * P, P, range(2))
+        def part_x(c, m0, w):
+            last[c, m0] = bank("last")
+            stage2(c, last[c, m0][:, :w], m0, w, range(2))
 
-        def last_k(q):
-            stage2(7, last[q][:, :P], q * P, P, range(2, 4))
+        def part_k(c, m0, w):
+            stage2(c, last[c, m0][:, :w], m0, w, range(2, 4))
 
-        def copy_last(q):
-            nc.scalar.copy(out=y_sb[1][:, 3, q * P : (q + 1) * P], in_=last[q][:, :P])
+        def copy_part(c, m0, w):
+            nc.scalar.copy(out=y_sb[c // 4][:, c % 4, m0 : m0 + w], in_=last[c, m0][:, :w])
 
-        def copy_last_v(q):
-            nc.vector.tensor_copy(out=y_sb[1][:, 3, q * P : (q + 1) * P], in_=last[q][:, :P])
+        def copy_part_v(c, m0, w):
+            nc.vector.tensor_copy(out=y_sb[c // 4][:, c % 4, m0 : m0 + w], in_=last[c, m0][:, :w])
 
-        def store_y_last():
-            nc.sync.dma_start(out=o_v[1][:, 3, :], in_=y_sb[1][:, 3, :])
+        def store_part(c, m0, w):
+            nc.sync.dma_start(out=o_v[c // 4][:, c % 4, m0 : m0 + w], in_=y_sb[c // 4][:, c % 4, m0 : m0 + w])
 
         def cast_k2_v(c):
             nc.vector.tensor_copy(out=kb[c][:, 0:512], in_=k2f[c][:])
@@ -241,7 +259,8 @@ def tile_factoredcubicvolterraequalizer_x2_kernel(
 
         def store_scales(g):
             for q in range(4):
-                nc.sync.dma_start(
+                eng = nc.scalar if g == 1 and q < 2 else nc.sync
+                eng.dma_start(
                     out=out_2[g, 4 * q : 4 * q + 4, :].bitcast(I32), in_=y_pl[g][32 * q : 32 * q + 4, :].bitcast(I32)
                 )
 
@@ -249,139 +268,158 @@ def tile_factoredcubicvolterraequalizer_x2_kernel(
             stage1(c, a_cod, 0, pb, "pb")
 
         def q_of(c):
-            stage1(c, b_cod, 8, qb, "qb")
+            stage1(c, b_cod, 1, qb, "qb")
 
-        transpose_x(0)
-        copy_x(0)
-        perm(a_cod, a_raw)
-        transpose_x(1)
-        copy_x(1)
+        def warm_up(count):
+            wb = bank("wb")
+            for i in range(count):
+                nc.tensor.matmul_mx(
+                    out=wb[:, 0:P],
+                    lhsT=warm_cod[:].bitcast(FP8X4),
+                    lhsT_scale=warm_pl[:],
+                    rhs=warm_cod[:].bitcast(FP8X4),
+                    rhs_scale=warm_pl[:],
+                    start=True,
+                    stop=True,
+                )
+
+        warm_up(8)
+        perm_scales(0)
+        transpose_x(0, (0,))
+        copy_x_half(0, 0)
+        perm(a_cod, a_raw, 0, 2)
+        transpose_x(0, (1,))
+        copy_x_half(0, 1)
         quant_x(0)
-        perm_scales()
+        warm_up(12)
+        perm(a_cod, a_raw, 2, 4)
         p_of(0)
         copy_p(0)
+        perm(b_cod, b_raw, 0, 2)
+        transpose_x(1)
+        copy_x(1)
+        perm_scales(1)
+        perm(b_cod, b_raw, 2, 4)
+        q_of(0)
         quant_x(1)
         transpose_x(2)
         copy_x(2)
-        perm(b_cod, b_raw)
+        make_k2(0)
         transpose_x(3)
         copy_x(3)
         quant_x(2)
         p_of(1)
         copy_p(1)
         quant_x(3)
-        q_of(0)
-        make_k2(0)
         q_of(1)
         cast_k2(0)
-        make_k3(0)
+        make_k2(1)
         p_of(2)
         copy_p(2)
-        make_k2(1)
+        make_k3(0)
         q_of(2)
         cast_k2(1)
-        quant_k(0)
+        make_k2(2)
         transpose_x(4)
         copy_x(4)
         make_k3(1)
         transpose_x(5)
         copy_x(5)
-        quant_k(1)
+        quant_k(0)
+        transpose_x(6)
+        copy_x(6)
+        quant_x(4)
+        transpose_x(7)
+        copy_x(7)
+        quant_x(5)
         p_of(3)
         copy_p(3)
-        make_k2(2)
+        quant_x(6)
         q_of(3)
         cast_k2(2)
-        quant_x(4)
-        stage2_wide(0)
-        copy_y(0)
-        make_k3(2)
-        store_y(0)
+        quant_x(7)
         p_of(4)
         copy_p(4)
-        quant_x(5)
+        make_k3(2)
         q_of(4)
-        quant_k(2)
-        transpose_x(6)
-        make_k2(3)
-        transpose_x(7)
-        cast_k2(3)
-        make_k3(3)
-        stage2_wide(1)
-        copy_x(6)
-        quant_k(3)
+        quant_k(1)
         p_of(5)
-        copy_x(7)
-        make_k2(4)
+        make_k2(3)
         q_of(5)
-        copy_y(1)
-        quant_x(6)
-        store_y(1)
-        stage2_wide(2)
+        cast_k2(3)
+        quant_k(2)
+        stage2_wide(0)
         copy_p(5)
-        make_k3(4)
+        make_k2(4)
         p_of(6)
         cast_k2(4)
-        quant_x(7)
+        make_k3(3)
         q_of(6)
-        copy_y(2)
-        quant_k(4)
-        store_y(2)
-        stage2_wide(3)
-        copy_p(6)
+        copy_y(0)
         make_k2(5)
+        store_y(0)
+        stage2_wide(1)
+        copy_p(6)
+        make_k3(4)
         p_of(7)
         cast_k2(5)
-        make_k3(5)
+        quant_k(3)
         q_of(7)
+        copy_y(1)
+        make_k2(6)
+        store_y(1)
+        stage2_wide(2)
+        copy_p(7)
+        make_k3(5)
+        stage2_wide(3)
+        cast_k2(6)
+        quant_k(4)
+        stage2_wide(4)
+        copy_y(2)
+        make_k2(7)
+        store_y(2)
+        cast_k2(7)
+        make_k3(6)
         copy_y(3)
         quant_k(5)
         store_y(3)
-        stage2_wide(4)
-        copy_p(7)
-        make_k2(6)
         stage2_wide(5)
-        cast_k2(6)
-        make_k3(6)
         copy_y(4)
-        quant_k(6)
-        store_y(4)
-        stage2_wide(6)
-        make_k2(7)
-        last_x(0)
-        cast_k2(7)
-        interleave_y(0, 0, 256, "vector")
-        last_x(1)
-        copy_y(5)
         make_k3(7)
-        store_y(5)
-        last_x(2)
-        copy_y(6)
-        quant_y(0, 0, 256)
-        store_y(6)
-        last_x(3)
+        store_y(4)
+        part_x(6, 0, 256)
+        copy_y(5)
+        quant_k(6)
+        part_k(6, 0, 256)
+        copy_part(6, 0, 256)
+        interleave_y(0, 0, 256, "vector")
+        part_x(7, 0, 256)
         quant_k(7)
-        last_k(0)
-        copy_last(0)
+        part_k(7, 0, 256)
+        copy_part(7, 0, 256)
         interleave_y(0, 256, 256, "vector")
-        last_k(1)
-        copy_last(1)
+        part_x(6, 256, 256)
+        quant_y(0, 0, 256)
+        part_k(6, 256, 256)
+        copy_part(6, 256, 256)
         quant_y(0, 256, 256)
         store_codes(0, 0, 512)
-        last_k(2)
-        copy_last(2)
-        interleave_y(1, 0, 128, "vector")
+        part_x(7, 256, 128)
+        interleave_y(1, 0, 256, "vector")
         store_scales(0)
-        last_k(3)
-        copy_last(3)
-        interleave_y(1, 128, 128, "vector")
-        store_y_last()
-        interleave_y(1, 384, 128, "scalar")
-        quant_y(1, 0, 128)
+        part_k(7, 256, 128)
+        copy_part(7, 256, 128)
         interleave_y(1, 256, 128, "vector")
-        quant_y(1, 128, 128)
-        store_codes(1, 0, 256)
+        store_y(5)
+        part_x(7, 384, 128)
+        quant_y(1, 0, 256)
+        store_part(6, 0, 512)
+        part_k(7, 384, 128)
+        copy_part(7, 384, 128)
+        interleave_y(1, 384, 128, "vector")
+        store_part(7, 0, 512)
         quant_y(1, 256, 128)
+        store_codes(1, 0, 256)
         quant_y(1, 384, 128)
         store_codes(1, 256, 256)
         store_scales(1)

@@ -29,7 +29,8 @@ def tile_factoredcubicvolterraequalizer_x2_kernel(
         ctx.enter_context(tc.manual_schedule())
 
         ident = keep.tile([P, P], F32, align_bytes=64)
-        raw_pl = [keep.tile([P, 512], U8, align_bytes=64, name="raw_pl%d" % i) for i in range(2)]
+        raw_both = keep.tile([P, 2, 512], U8, align_bytes=64)
+        raw_pl = [raw_both[:, i, :] for i in range(2)]
         perm_pl = [keep.tile([P, 512], U8, align_bytes=64, name="perm_pl%d" % i) for i in range(2)]
         h_pl = keep.tile([P, 512], U8, align_bytes=64)
         a_raw = keep.tile([P, 2, 512], I32, align_bytes=64)
@@ -55,17 +56,16 @@ def tile_factoredcubicvolterraequalizer_x2_kernel(
         x_v = [x[512 * g : 512 * g + 512, :].rearrange("(p t) k -> p t k", t=4) for g in range(2)]
         o_v = [out_0[512 * g : 512 * g + 512, :].rearrange("(p t) m -> p t m", t=4) for g in range(2)]
 
-        nc.vector.memset(raw_pl[0][:].bitcast(I32), 0)
+        nc.vector.memset(raw_both[:].rearrange("p i n -> p (i n)").bitcast(I32), 0)
         zero = keep.tile([P, 512], BF16, align_bytes=64)
         warm_cod = keep.tile([P, P], I32, align_bytes=64)
         warm_pl = keep.tile([P, P], U8, align_bytes=64)
         nc.vector.memset(zero[:].bitcast(I32), 0)
-        nc.vector.memset(raw_pl[1][:].bitcast(I32), 0)
         nc.vector.quantize_mx(out=warm_cod[:].bitcast(FP8X4), scales=warm_pl[:], in_=zero[:])
         nc.vector.memset(h_pl[:].bitcast(I32), 0)
 
-        def load_x(c, count, k0=0, k1=N):
-            nc.sync.dma_start(
+        def load_x(eng, c, count, k0=0, k1=N):
+            eng.dma_start(
                 out=x_raw[c][0][:, :, k0:k1], in_=x_v[c // 4][:, c % 4 : c % 4 + count, k0:k1]
             )
 
@@ -81,23 +81,22 @@ def tile_factoredcubicvolterraequalizer_x2_kernel(
                     in_=scales[:, 4 * q : 4 * q + 4, :].bitcast(I32),
                 )
 
-        load_x(0, 1, 0, 512)
-        load_x(0, 1, 512, N)
-        load_s(nc.scalar, raw_pl[0], 0, a_scales)
-        load_w(nc.scalar, a_raw[:], a_words)
-        load_s(nc.sync, raw_pl[1], 0, b_scales)
-        load_w(nc.gpsimd, b_raw[:], b_words)
+        load_x(nc.sync, 0, 1)
+        load_s(nc.sync, raw_pl[0], 0, a_scales)
+        load_x(nc.sync, 1, 1)
+        load_x(nc.sync, 2, 2)
+        load_w(nc.sync, a_raw[:], a_words)
         make_identity(nc, ident[:])
-        load_x(1, 1)
-        load_x(2, 2)
+        load_s(nc.sync, raw_pl[1], 0, b_scales)
+        load_w(nc.sync, b_raw[:], b_words)
+        load_x(nc.sync, 4, 2)
+        load_x(nc.sync, 6, 2)
         load_w(nc.sync, h_cod[:, 0:2, :], h1_words)
-        load_x(4, 2)
-        load_x(6, 2)
-        load_w(nc.sync, h_cod[:, 2:3, :], h2_words)
-        load_w(nc.sync, h_cod[:, 3:4, :], h3_words)
         load_s(nc.sync, h_pl, 0, h1_scales)
         load_s(nc.sync, h_pl, 8, h2_scales)
         load_s(nc.sync, h_pl, 12, h3_scales)
+        load_w(nc.sync, h_cod[:, 2:3, :], h2_words)
+        load_w(nc.sync, h_cod[:, 3:4, :], h3_words)
 
         def bank(nm):
             return psum.tile([P, 512], F32, tag="bank", name=nm)
@@ -142,7 +141,7 @@ def tile_factoredcubicvolterraequalizer_x2_kernel(
         def perm_scales(i):
             nc.vector.tensor_copy(
                 out=perm_pl[i][:].rearrange("p (t m) -> p t m", t=4),
-                in_=raw_pl[i][:].rearrange("p (m t) -> p t m", t=4),
+                in_=raw_pl[i].rearrange("p (m t) -> p t m", t=4),
             )
 
         def stage1(c, cod, i, banks, nm):
@@ -284,121 +283,120 @@ def tile_factoredcubicvolterraequalizer_x2_kernel(
                 )
 
         warm_up(8)
-        perm_scales(0)
-        transpose_x(0, (0,))
-        copy_x_half(0, 0)
-        perm(a_cod, a_raw, 0, 2)
-        transpose_x(0, (1,))
-        copy_x_half(0, 1)
+        transpose_x(0)
+        copy_x(0)
         quant_x(0)
-        warm_up(12)
-        perm(a_cod, a_raw, 2, 4)
-        p_of(0)
-        copy_p(0)
-        perm(b_cod, b_raw, 0, 2)
         transpose_x(1)
         copy_x(1)
-        perm_scales(1)
-        perm(b_cod, b_raw, 2, 4)
-        q_of(0)
+        perm_scales(0)
+        warm_up(6)
         quant_x(1)
         transpose_x(2)
         copy_x(2)
-        make_k2(0)
+        perm(a_cod, a_raw, 0, 2)
         transpose_x(3)
         copy_x(3)
+        perm(a_cod, a_raw, 2, 4)
+        warm_up(6)
         quant_x(2)
+        p_of(0)
+        copy_p(0)
+        quant_x(3)
         p_of(1)
         copy_p(1)
-        quant_x(3)
+        perm_scales(1)
+        p_of(2)
+        copy_p(2)
+        perm(b_cod, b_raw, 0, 2)
+        perm(b_cod, b_raw, 2, 4)
+        q_of(0)
+        make_k2(0)
         q_of(1)
         cast_k2(0)
         make_k2(1)
-        p_of(2)
-        copy_p(2)
-        make_k3(0)
         q_of(2)
         cast_k2(1)
-        make_k2(2)
+        make_k3(0)
         transpose_x(4)
         copy_x(4)
-        make_k3(1)
+        make_k2(2)
         transpose_x(5)
         copy_x(5)
-        quant_k(0)
+        make_k3(1)
         transpose_x(6)
-        copy_x(6)
+        cast_k2(2)
         quant_x(4)
         transpose_x(7)
+        copy_x(6)
+        quant_k(0)
+        p_of(3)
         copy_x(7)
         quant_x(5)
-        p_of(3)
-        copy_p(3)
-        quant_x(6)
         q_of(3)
-        cast_k2(2)
-        quant_x(7)
+        copy_p(3)
+        make_k3(2)
         p_of(4)
         copy_p(4)
-        make_k3(2)
-        q_of(4)
         quant_k(1)
+        q_of(4)
+        quant_x(6)
         p_of(5)
-        make_k2(3)
+        quant_x(7)
         q_of(5)
-        cast_k2(3)
         quant_k(2)
+        p_of(6)
+        make_k2(3)
+        q_of(6)
+        cast_k2(3)
+        make_k2(4)
         stage2_wide(0)
         copy_p(5)
-        make_k2(4)
-        p_of(6)
-        cast_k2(4)
         make_k3(3)
-        q_of(6)
-        copy_y(0)
+        p_of(7)
+        cast_k2(4)
         make_k2(5)
-        store_y(0)
-        stage2_wide(1)
+        q_of(7)
         copy_p(6)
         make_k3(4)
-        p_of(7)
+        stage2_wide(1)
         cast_k2(5)
         quant_k(3)
-        q_of(7)
-        copy_y(1)
-        make_k2(6)
-        store_y(1)
         stage2_wide(2)
+        copy_y(0)
+        make_k2(6)
+        store_y(0)
+        stage2_wide(3)
         copy_p(7)
         make_k3(5)
-        stage2_wide(3)
         cast_k2(6)
         quant_k(4)
         stage2_wide(4)
-        copy_y(2)
         make_k2(7)
-        store_y(2)
         cast_k2(7)
         make_k3(6)
-        copy_y(3)
+        copy_y(1)
         quant_k(5)
-        store_y(3)
+        store_y(1)
         stage2_wide(5)
-        copy_y(4)
+        copy_y(2)
         make_k3(7)
-        store_y(4)
+        store_y(2)
         part_x(6, 0, 256)
-        copy_y(5)
+        copy_y(3)
         quant_k(6)
+        store_y(3)
         part_k(6, 0, 256)
-        copy_part(6, 0, 256)
-        interleave_y(0, 0, 256, "vector")
-        part_x(7, 0, 256)
+        copy_y(4)
         quant_k(7)
+        store_y(4)
+        part_x(7, 0, 256)
+        copy_y(5)
+        interleave_y(0, 0, 256, "vector")
         part_k(7, 0, 256)
-        copy_part(7, 0, 256)
+        copy_part(6, 0, 256)
         interleave_y(0, 256, 256, "vector")
         part_x(6, 256, 256)
+        copy_part(7, 0, 256)
         quant_y(0, 0, 256)
         part_k(6, 256, 256)
         copy_part(6, 256, 256)

@@ -15,6 +15,7 @@ FLOPS = 2 * T * (N * R * 2 + N * O + R * O * 2)
 P = 128
 PACK = 4
 KP = 512
+PERMUTED_FROM = 4
 
 
 def tile_factoredcubicvolterraequalizer_x2_kernel(
@@ -45,8 +46,12 @@ def tile_factoredcubicvolterraequalizer_x2_kernel(
         for c in range(2, 8, 2):
             x_two = keep.tile([P, 2, N], BF16, align_bytes=64, name="x_two%d" % c)
             x_raw.extend([(x_two, 0), (x_two, 1)])
-        x_cod = [keep.tile([P, 256], I32, align_bytes=64, name="x_cod%d" % c) for c in range(8)]
-        x_pl = [keep.tile([P, 256], U8, align_bytes=64, name="x_pl%d" % c) for c in range(8)]
+        x_cod = [keep.tile([P, 2, 256], I32, align_bytes=64, name="x_cod%d" % d) for d in range(4)]
+        x_pl = [keep.tile([P, 2, 256], U8, align_bytes=64, name="x_pl%d" % d) for d in range(4)]
+        xb = [keep.tile([P, 2, 256, 4], BF16, align_bytes=64, name="xb%d" % d) for d in range(4)]
+        x_perm = [keep.tile([P, 2, 512], F32, align_bytes=64, name="x_perm%d" % i) for i in range(2)]
+        psb = [keep.tile([P, 2, 256, 2], F32, align_bytes=64, name="psb%d" % d) for d in range(4)]
+        k2f = [keep.tile([P, 2, 256, 2], F32, align_bytes=64, name="k2f%d" % d) for d in range(4)]
         k_cod = [keep.tile([P, 256], I32, align_bytes=64, name="k_cod%d" % c) for c in range(8)]
         k_pl = [keep.tile([P, 256], U8, align_bytes=64, name="k_pl%d" % c) for c in range(8)]
         y_sb = [keep.tile([P, 4, 512], F32, align_bytes=64, name="y_sb%d" % g) for g in range(2)]
@@ -101,36 +106,39 @@ def tile_factoredcubicvolterraequalizer_x2_kernel(
         def bank(nm):
             return psum.tile([P, 512], F32, tag="bank", name=nm)
 
-        xt, xb, pb, qb, psb, k2f, kb = {}, {}, {}, {}, {}, {}, {}
+        xt, pb, qb, kb = {}, {}, {}, {}
 
-        def transpose_x(c, groups=(0, 1)):
-            if 0 in groups:
-                xt[c] = bank("xt")
-            words = x_raw[c][0][:, x_raw[c][1], :].bitcast(F32)
-            for g in groups:
-                for u in range(2):
-                    col = (2 * g + u) * P
-                    nc.tensor.transpose(
-                        xt[c][:, col : col + P], words[:, 256 * g + u : 256 * (g + 1) : 2], ident[:]
-                    )
-
-        def copy_x_half(c, g):
-            if g == 0:
-                xb[c] = work.tile([P, N], BF16, align_bytes=64, tag="xb", name="xb")
-            nc.scalar.copy(
-                out=xb[c][:, 512 * g : 512 * (g + 1)].bitcast(F32).rearrange("p (r u) -> p r u", u=2),
-                in_=xt[c][:, 256 * g : 256 * (g + 1)].rearrange("p (u r) -> p r u", u=2),
+        def permute_words(i):
+            nc.vector.tensor_copy(
+                out=x_perm[i][:].rearrange("p s (g u k) -> p (s g) u k", g=2, u=2),
+                in_=x_raw[4 + 2 * i][0][:].bitcast(F32).rearrange("p s (g k u) -> p (s g) u k", g=2, u=2),
             )
 
+        def transpose_x(c):
+            xt[c] = bank("xt")
+            for g in range(2):
+                for u in range(2):
+                    col = (2 * g + u) * P
+                    if c < PERMUTED_FROM:
+                        words = x_raw[c][0][:, x_raw[c][1], :].bitcast(F32)
+                        in_ = words[:, 256 * g + u : 256 * (g + 1) : 2]
+                    else:
+                        in_ = x_perm[(c - 4) // 2][:, c % 2, col : col + P]
+                    nc.tensor.transpose(xt[c][:, col : col + P], in_, ident[:])
+
         def copy_x(c):
-            xb[c] = work.tile([P, N], BF16, align_bytes=64, tag="xb", name="xb")
+            d, half = divmod(c, 2)
             nc.scalar.copy(
-                out=xb[c][:].bitcast(F32).rearrange("p (g r u) -> p g r u", g=2, u=2),
+                out=xb[d][:, :, half * P : (half + 1) * P, :].rearrange("p g r e -> p g (r e)").bitcast(F32).rearrange("p g (r u) -> p g r u", u=2),
                 in_=xt[c][:].rearrange("p (g u r) -> p g r u", g=2, u=2),
             )
 
-        def quant_x(c):
-            nc.vector.quantize_mx(out=x_cod[c][:].bitcast(FP8X4), scales=x_pl[c][:], in_=xb[c][:])
+        def quant_x(d):
+            nc.vector.quantize_mx(
+                out=x_cod[d][:].rearrange("p g r -> p (g r)").bitcast(FP8X4),
+                scales=x_pl[d][:].rearrange("p g r -> p (g r)"),
+                in_=xb[d][:].rearrange("p g r e -> p (g r e)"),
+            )
 
         def perm(cod, raw, t0, t1):
             nc.vector.tensor_copy(
@@ -144,58 +152,77 @@ def tile_factoredcubicvolterraequalizer_x2_kernel(
                 in_=raw_pl[i].rearrange("p (m t) -> p t m", t=4),
             )
 
-        def stage1(c, cod, i, banks, nm):
-            banks[c] = bank(nm)
-            for t in range(4):
+        def stage1(d, h, cod, i, banks, nm):
+            banks[d, h] = bank(nm)
+            for j in range(2):
+                t = 2 * h + j
                 for g in range(2):
                     nc.tensor.matmul_mx(
-                        out=banks[c][:, t * P : (t + 1) * P],
+                        out=banks[d, h][:, j * 256 : (j + 1) * 256],
                         lhsT=cod[:, g, t * P : (t + 1) * P].bitcast(FP8X4),
                         lhsT_scale=perm_pl[i][4 * g : P, t * P : (t + 1) * P],
-                        rhs=x_cod[c][:, g * P : (g + 1) * P].bitcast(FP8X4),
-                        rhs_scale=x_pl[c][:, g * P : (g + 1) * P],
+                        rhs=x_cod[d][:, g, :].bitcast(FP8X4),
+                        rhs_scale=x_pl[d][:, g, :],
                         start=(g == 0),
                         stop=(g == 1),
                     )
 
-        def copy_p(c):
-            psb[c] = work.tile([P, 512], F32, align_bytes=64, tag="psb", name="psb")
-            nc.scalar.copy(
-                out=psb[c][:].rearrange("p (n t) -> p n t", t=4),
-                in_=pb[c][:].rearrange("p (t n) -> p n t", t=4),
-            )
+        def copy_p(d, h):
+            nc.scalar.copy(out=psb[d][:, h, :, :], in_=pb[d, h][:].rearrange("p (j n) -> p n j", j=2))
 
-        def make_k2(c):
-            k2f[c] = work.tile([P, 512], F32, align_bytes=64, tag="k2f", name="k2f")
+        def make_k2(d, h):
             nc.vector.tensor_tensor(
-                out=k2f[c][:].rearrange("p (n t) -> p n t", t=4),
-                in0=qb[c][:].rearrange("p (t n) -> p n t", t=4),
-                in1=psb[c][:].rearrange("p (n t) -> p n t", t=4),
+                out=k2f[d][:, h, :, :],
+                in0=qb[d, h][:].rearrange("p (j n) -> p n j", j=2),
+                in1=psb[d][:, h, :, :],
                 op=MULT,
             )
-            kb[c] = work.tile([P, 1024], BF16, align_bytes=64, tag="kb", name="kb")
+
+        def tokens(tile, c):
+            d, half = divmod(c, 2)
+            return tile[d][:, :, half * P : (half + 1) * P, :].rearrange("p h n j -> p n h j")
+
+        def k_tile(c):
+            if c not in kb:
+                kb[c] = work.tile([P, 2, P, 2, 2], BF16, align_bytes=64, tag="kb", name="kb")
+            return kb[c]
 
         def make_k3(c):
-            nc.vector.tensor_tensor(out=kb[c][:, 512:1024], in0=k2f[c][:], in1=psb[c][:], op=MULT)
+            nc.vector.tensor_tensor(out=k_tile(c)[:, 1, :, :, :], in0=tokens(k2f, c), in1=tokens(psb, c), op=MULT)
 
         def cast_k2(c):
-            nc.scalar.copy(out=kb[c][:, 0:512], in_=k2f[c][:])
+            nc.scalar.copy(out=k_tile(c)[:, 0, :, :, :], in_=tokens(k2f, c))
 
         def quant_k(c):
-            nc.vector.quantize_mx(out=k_cod[c][:].bitcast(FP8X4), scales=k_pl[c][:], in_=kb[c][:])
+            nc.vector.quantize_mx(
+                out=k_cod[c][:].bitcast(FP8X4),
+                scales=k_pl[c][:],
+                in_=kb[c][:].rearrange("p i n h j -> p (i n h j)"),
+            )
 
+        def x_columns(tile, c, g):
+            d, half = divmod(c, 2)
+            return tile[d][:, g, half * P : (half + 1) * P]
 
-        stage2_operands = [(x_cod, x_pl, 0, 0), (x_cod, x_pl, 1, 1), (k_cod, k_pl, 0, 2), (k_cod, k_pl, 1, 3)]
+        def k_columns(tile, c, i):
+            return tile[c][:, i * P : (i + 1) * P]
+
+        stage2_operands = [
+            (x_columns, x_cod, x_pl, 0),
+            (x_columns, x_cod, x_pl, 1),
+            (k_columns, k_cod, k_pl, 0),
+            (k_columns, k_cod, k_pl, 1),
+        ]
 
         def stage2(c, out_ap, m0, width, passes):
             for i in passes:
-                cod, pl, half, h = stage2_operands[i]
+                columns, cod, pl, half = stage2_operands[i]
                 nc.tensor.matmul_mx(
                     out=out_ap,
-                    lhsT=cod[c][:, half * P : (half + 1) * P].bitcast(FP8X4),
-                    lhsT_scale=pl[c][:, half * P : (half + 1) * P],
-                    rhs=h_cod[:, h, m0 : m0 + width].bitcast(FP8X4),
-                    rhs_scale=h_pl[4 * h : P, m0 : m0 + width],
+                    lhsT=columns(cod, c, half).bitcast(FP8X4),
+                    lhsT_scale=columns(pl, c, half),
+                    rhs=h_cod[:, i, m0 : m0 + width].bitcast(FP8X4),
+                    rhs_scale=h_pl[4 * i : P, m0 : m0 + width],
                     start=(i == 0),
                     stop=(i == 3),
                 )
@@ -232,9 +259,6 @@ def tile_factoredcubicvolterraequalizer_x2_kernel(
         def store_part(c, m0, w):
             nc.sync.dma_start(out=o_v[c // 4][:, c % 4, m0 : m0 + w], in_=y_sb[c // 4][:, c % 4, m0 : m0 + w])
 
-        def cast_k2_v(c):
-            nc.vector.tensor_copy(out=kb[c][:, 0:512], in_=k2f[c][:])
-
         def interleave_y(g, m0, width, engine):
             yb[g, m0] = work.tile([P, 1024], BF16, align_bytes=64, tag="yb", name="yb")
             copy = nc.scalar.copy if engine == "scalar" else nc.vector.tensor_copy
@@ -258,16 +282,16 @@ def tile_factoredcubicvolterraequalizer_x2_kernel(
 
         def store_scales(g):
             for q in range(4):
-                eng = nc.scalar if g == 1 and q < 2 else nc.sync
+                eng = nc.sync
                 eng.dma_start(
                     out=out_2[g, 4 * q : 4 * q + 4, :].bitcast(I32), in_=y_pl[g][32 * q : 32 * q + 4, :].bitcast(I32)
                 )
 
-        def p_of(c):
-            stage1(c, a_cod, 0, pb, "pb")
+        def p_of(d, h):
+            stage1(d, h, a_cod, 0, pb, "pb")
 
-        def q_of(c):
-            stage1(c, b_cod, 1, qb, "qb")
+        def q_of(d, h):
+            stage1(d, h, b_cod, 1, qb, "qb")
 
         def warm_up(count):
             wb = bank("wb")
@@ -283,120 +307,118 @@ def tile_factoredcubicvolterraequalizer_x2_kernel(
                 )
 
         warm_up(8)
+        perm_scales(0)
         transpose_x(0)
         copy_x(0)
-        quant_x(0)
         transpose_x(1)
         copy_x(1)
-        perm_scales(0)
-        warm_up(6)
-        quant_x(1)
+        quant_x(0)
+        warm_up(8)
+        perm(a_cod, a_raw, 0, 2)
         transpose_x(2)
         copy_x(2)
-        perm(a_cod, a_raw, 0, 2)
+        perm(a_cod, a_raw, 2, 4)
         transpose_x(3)
         copy_x(3)
-        perm(a_cod, a_raw, 2, 4)
-        warm_up(6)
-        quant_x(2)
-        p_of(0)
-        copy_p(0)
-        quant_x(3)
-        p_of(1)
-        copy_p(1)
+        quant_x(1)
+        warm_up(8)
         perm_scales(1)
-        p_of(2)
-        copy_p(2)
+        p_of(0, 0)
+        copy_p(0, 0)
         perm(b_cod, b_raw, 0, 2)
+        p_of(0, 1)
+        copy_p(0, 1)
         perm(b_cod, b_raw, 2, 4)
-        q_of(0)
-        make_k2(0)
-        q_of(1)
-        cast_k2(0)
-        make_k2(1)
-        q_of(2)
-        cast_k2(1)
-        make_k3(0)
+        p_of(1, 0)
+        copy_p(1, 0)
+        permute_words(0)
+        p_of(1, 1)
+        copy_p(1, 1)
+        q_of(0, 0)
+        make_k2(0, 0)
+        q_of(0, 1)
+        make_k2(0, 1)
         transpose_x(4)
         copy_x(4)
-        make_k2(2)
+        permute_words(1)
         transpose_x(5)
         copy_x(5)
-        make_k3(1)
+        make_k3(0)
+        q_of(1, 0)
+        cast_k2(0)
+        quant_x(2)
+        q_of(1, 1)
+        cast_k2(1)
+        make_k2(1, 0)
         transpose_x(6)
-        cast_k2(2)
-        quant_x(4)
-        transpose_x(7)
         copy_x(6)
-        quant_k(0)
-        p_of(3)
+        make_k2(1, 1)
+        transpose_x(7)
         copy_x(7)
-        quant_x(5)
-        q_of(3)
-        copy_p(3)
-        make_k3(2)
-        p_of(4)
-        copy_p(4)
-        quant_k(1)
-        q_of(4)
-        quant_x(6)
-        p_of(5)
-        quant_x(7)
-        q_of(5)
-        quant_k(2)
-        p_of(6)
-        make_k2(3)
-        q_of(6)
+        make_k3(1)
+        p_of(2, 0)
+        copy_p(2, 0)
+        quant_x(3)
+        p_of(2, 1)
+        copy_p(2, 1)
+        quant_k(0)
+        q_of(2, 0)
+        cast_k2(2)
+        make_k2(2, 0)
+        q_of(2, 1)
         cast_k2(3)
-        make_k2(4)
-        stage2_wide(0)
-        copy_p(5)
-        make_k3(3)
-        p_of(7)
+        make_k2(2, 1)
+        p_of(3, 0)
+        copy_p(3, 0)
+        quant_k(1)
+        p_of(3, 1)
+        copy_p(3, 1)
+        make_k3(2)
+        q_of(3, 0)
         cast_k2(4)
-        make_k2(5)
-        q_of(7)
-        copy_p(6)
-        make_k3(4)
-        stage2_wide(1)
+        make_k3(3)
+        q_of(3, 1)
         cast_k2(5)
-        quant_k(3)
-        stage2_wide(2)
+        make_k2(3, 0)
+        stage2_wide(0)
         copy_y(0)
-        make_k2(6)
+        make_k2(3, 1)
         store_y(0)
-        stage2_wide(3)
-        copy_p(7)
-        make_k3(5)
+        stage2_wide(1)
         cast_k2(6)
-        quant_k(4)
-        stage2_wide(4)
-        make_k2(7)
+        quant_k(2)
+        stage2_wide(2)
         cast_k2(7)
-        make_k3(6)
+        quant_k(3)
+        stage2_wide(3)
         copy_y(1)
-        quant_k(5)
+        make_k3(4)
         store_y(1)
-        stage2_wide(5)
         copy_y(2)
-        make_k3(7)
+        make_k3(5)
         store_y(2)
-        part_x(6, 0, 256)
         copy_y(3)
-        quant_k(6)
+        quant_k(4)
         store_y(3)
-        part_k(6, 0, 256)
+        stage2_wide(4)
         copy_y(4)
-        quant_k(7)
+        make_k3(6)
         store_y(4)
-        part_x(7, 0, 256)
+        quant_k(5)
+        stage2_wide(5)
         copy_y(5)
+        make_k3(7)
+        part_x(6, 0, 256)
+        quant_k(6)
+        part_k(6, 0, 256)
+        copy_part(6, 0, 256)
+        quant_k(7)
+        part_x(7, 0, 256)
         interleave_y(0, 0, 256, "vector")
         part_k(7, 0, 256)
-        copy_part(6, 0, 256)
+        copy_part(7, 0, 256)
         interleave_y(0, 256, 256, "vector")
         part_x(6, 256, 256)
-        copy_part(7, 0, 256)
         quant_y(0, 0, 256)
         part_k(6, 256, 256)
         copy_part(6, 256, 256)

from contextlib import ExitStack

import concourse.mybir as mybir
from concourse.masks import make_identity

F32 = mybir.dt.float32
BF16 = mybir.dt.bfloat16
I32 = mybir.dt.int32
U8 = mybir.dt.uint8
FP8X4 = mybir.dt.float8_e4m3fn_x4
MULT = mybir.AluOpType.mult

T, N, R, O = 1024, 1024, 512, 512
FLOPS = 2 * T * (N * R * 2 + N * O + R * O * 2)
P = 128
PACK = 4
KP = 512
PERMUTED_FROM = 4


def tile_factoredcubicvolterraequalizer_x2_kernel(
    tc, x, a_words, a_scales, b_words, b_scales, h1_words, h1_scales,
    h2_words, h2_scales, h3_words, h3_scales, out_0, out_1, out_2,
):
    nc = tc.nc
    with ExitStack() as ctx:
        keep = ctx.enter_context(tc.tile_pool(name="keep", bufs=1))
        work = ctx.enter_context(tc.tile_pool(name="work", bufs=4))
        psum = ctx.enter_context(tc.psum_pool(name="psum", bufs=8))
        ctx.enter_context(tc.manual_schedule())

        ident = keep.tile([P, P], F32, align_bytes=64)
        raw_both = keep.tile([P, 2, 512], U8, align_bytes=64)
        raw_pl = [raw_both[:, i, :] for i in range(2)]
        perm_pl = [keep.tile([P, 512], U8, align_bytes=64, name="perm_pl%d" % i) for i in range(2)]
        h_pl = keep.tile([P, 512], U8, align_bytes=64)
        a_raw = keep.tile([P, 2, 512], I32, align_bytes=64)
        b_raw = keep.tile([P, 2, 512], I32, align_bytes=64)
        a_cod = keep.tile([P, 2, 512], I32, align_bytes=64)
        b_cod = keep.tile([P, 2, 512], I32, align_bytes=64)
        h_cod = keep.tile([P, 4, 512], I32, align_bytes=64)
        x_raw = []
        for c in range(2):
            x_one = keep.tile([P, 1, N], BF16, align_bytes=64, name="x_one%d" % c)
            x_raw.append((x_one, 0))
        for c in range(2, 8, 2):
            x_two = keep.tile([P, 2, N], BF16, align_bytes=64, name="x_two%d" % c)
            x_raw.extend([(x_two, 0), (x_two, 1)])
        x_cod = [keep.tile([P, 2, 256], I32, align_bytes=64, name="x_cod%d" % d) for d in range(4)]
        x_pl = [keep.tile([P, 2, 256], U8, align_bytes=64, name="x_pl%d" % d) for d in range(4)]
        xb = [keep.tile([P, 2, 256, 4], BF16, align_bytes=64, name="xb%d" % d) for d in range(4)]
        x_perm = [keep.tile([P, 2, 512], F32, align_bytes=64, name="x_perm%d" % i) for i in range(2)]
        psb = [keep.tile([P, 2, 256, 2], F32, align_bytes=64, name="psb%d" % d) for d in range(4)]
        k2f = [keep.tile([P, 2, 256, 2], F32, align_bytes=64, name="k2f%d" % d) for d in range(4)]
        k_cod = [keep.tile([P, 256], I32, align_bytes=64, name="k_cod%d" % c) for c in range(8)]
        k_pl = [keep.tile([P, 256], U8, align_bytes=64, name="k_pl%d" % c) for c in range(8)]
        y_sb = [keep.tile([P, 4, 512], F32, align_bytes=64, name="y_sb%d" % g) for g in range(2)]
        y_cod = [keep.tile([P, 512], I32, align_bytes=64, name="y_cod%d" % g) for g in range(2)]
        y_pl = [keep.tile([P, 512], U8, align_bytes=64, name="y_pl%d" % g) for g in range(2)]

        x_v = [x[512 * g : 512 * g + 512, :].rearrange("(p t) k -> p t k", t=4) for g in range(2)]
        o_v = [out_0[512 * g : 512 * g + 512, :].rearrange("(p t) m -> p t m", t=4) for g in range(2)]

        nc.vector.memset(raw_both[:].rearrange("p i n -> p (i n)").bitcast(I32), 0)
        zero = keep.tile([P, 512], BF16, align_bytes=64)
        warm_cod = keep.tile([P, P], I32, align_bytes=64)
        warm_pl = keep.tile([P, P], U8, align_bytes=64)
        nc.vector.memset(zero[:].bitcast(I32), 0)
        nc.vector.quantize_mx(out=warm_cod[:].bitcast(FP8X4), scales=warm_pl[:], in_=zero[:])
        nc.vector.memset(h_pl[:].bitcast(I32), 0)

        def load_x(eng, c, count, k0=0, k1=N):
            eng.dma_start(
                out=x_raw[c][0][:, :, k0:k1], in_=x_v[c // 4][:, c % 4 : c % 4 + count, k0:k1]
            )

        def load_w(eng, tile_ap, words):
            eng.dma_start(out=tile_ap, in_=words.rearrange("g p n t -> p g (n t)").bitcast(I32))

        def load_s(eng, plane, row, scales, quadrants=range(4)):
            passes = scales.shape[0]
            for q in quadrants:
                r0 = 32 * q + row
                eng.dma_start(
                    out=plane[r0 : r0 + 4 * passes, :].bitcast(I32),
                    in_=scales[:, 4 * q : 4 * q + 4, :].bitcast(I32),
                )

        load_x(nc.sync, 0, 1)
        load_s(nc.sync, raw_pl[0], 0, a_scales)
        load_x(nc.sync, 1, 1)
        load_x(nc.sync, 2, 2)
        load_w(nc.sync, a_raw[:], a_words)
        make_identity(nc, ident[:])
        load_s(nc.sync, raw_pl[1], 0, b_scales)
        load_w(nc.sync, b_raw[:], b_words)
        load_x(nc.sync, 4, 2)
        load_x(nc.sync, 6, 2)
        load_w(nc.sync, h_cod[:, 0:2, :], h1_words)
        load_s(nc.sync, h_pl, 0, h1_scales)
        load_s(nc.sync, h_pl, 8, h2_scales)
        load_s(nc.sync, h_pl, 12, h3_scales)
        load_w(nc.sync, h_cod[:, 2:3, :], h2_words)
        load_w(nc.sync, h_cod[:, 3:4, :], h3_words)

        def bank(nm):
            return psum.tile([P, 512], F32, tag="bank", name=nm)

        xt, pb, qb, kb = {}, {}, {}, {}

        def permute_words(i):
            nc.vector.tensor_copy(
                out=x_perm[i][:].rearrange("p s (g u k) -> p (s g) u k", g=2, u=2),
                in_=x_raw[4 + 2 * i][0][:].bitcast(F32).rearrange("p s (g k u) -> p (s g) u k", g=2, u=2),
            )

        def transpose_x(c):
            xt[c] = bank("xt")
            for g in range(2):
                for u in range(2):
                    col = (2 * g + u) * P
                    if c < PERMUTED_FROM:
                        words = x_raw[c][0][:, x_raw[c][1], :].bitcast(F32)
                        in_ = words[:, 256 * g + u : 256 * (g + 1) : 2]
                    else:
                        in_ = x_perm[(c - 4) // 2][:, c % 2, col : col + P]
                    nc.tensor.transpose(xt[c][:, col : col + P], in_, ident[:])

        def copy_x(c):
            d, half = divmod(c, 2)
            nc.scalar.copy(
                out=xb[d][:, :, half * P : (half + 1) * P, :].rearrange("p g r e -> p g (r e)").bitcast(F32).rearrange("p g (r u) -> p g r u", u=2),
                in_=xt[c][:].rearrange("p (g u r) -> p g r u", g=2, u=2),
            )

        def quant_x(d):
            nc.vector.quantize_mx(
                out=x_cod[d][:].rearrange("p g r -> p (g r)").bitcast(FP8X4),
                scales=x_pl[d][:].rearrange("p g r -> p (g r)"),
                in_=xb[d][:].rearrange("p g r e -> p (g r e)"),
            )

        def perm(cod, raw, t0, t1):
            nc.vector.tensor_copy(
                out=cod[:].rearrange("p g (t m) -> p g t m", t=4)[:, :, t0:t1, :],
                in_=raw[:].rearrange("p g (m t) -> p g t m", t=4)[:, :, t0:t1, :],
            )

        def perm_scales(i):
            nc.vector.tensor_copy(
                out=perm_pl[i][:].rearrange("p (t m) -> p t m", t=4),
                in_=raw_pl[i].rearrange("p (m t) -> p t m", t=4),
            )

        def stage1(d, h, cod, i, banks, nm):
            banks[d, h] = bank(nm)
            for j in range(2):
                t = 2 * h + j
                for g in range(2):
                    nc.tensor.matmul_mx(
                        out=banks[d, h][:, j * 256 : (j + 1) * 256],
                        lhsT=cod[:, g, t * P : (t + 1) * P].bitcast(FP8X4),
                        lhsT_scale=perm_pl[i][4 * g : P, t * P : (t + 1) * P],
                        rhs=x_cod[d][:, g, :].bitcast(FP8X4),
                        rhs_scale=x_pl[d][:, g, :],
                        start=(g == 0),
                        stop=(g == 1),
                    )

        def copy_p(d, h):
            nc.scalar.copy(out=psb[d][:, h, :, :], in_=pb[d, h][:].rearrange("p (j n) -> p n j", j=2))

        def make_k2(d, h):
            nc.vector.tensor_tensor(
                out=k2f[d][:, h, :, :],
                in0=qb[d, h][:].rearrange("p (j n) -> p n j", j=2),
                in1=psb[d][:, h, :, :],
                op=MULT,
            )

        def tokens(tile, c):
            d, half = divmod(c, 2)
            return tile[d][:, :, half * P : (half + 1) * P, :].rearrange("p h n j -> p n h j")

        def k_tile(c):
            if c not in kb:
                kb[c] = work.tile([P, 2, P, 2, 2], BF16, align_bytes=64, tag="kb", name="kb")
            return kb[c]

        def make_k3(c):
            nc.vector.tensor_tensor(out=k_tile(c)[:, 1, :, :, :], in0=tokens(k2f, c), in1=tokens(psb, c), op=MULT)

        def cast_k2(c):
            nc.scalar.copy(out=k_tile(c)[:, 0, :, :, :], in_=tokens(k2f, c))

        def quant_k(c):
            nc.vector.quantize_mx(
                out=k_cod[c][:].bitcast(FP8X4),
                scales=k_pl[c][:],
                in_=kb[c][:].rearrange("p i n h j -> p (i n h j)"),
            )

        def x_columns(tile, c, g):
            d, half = divmod(c, 2)
            return tile[d][:, g, half * P : (half + 1) * P]

        def k_columns(tile, c, i):
            return tile[c][:, i * P : (i + 1) * P]

        stage2_operands = [
            (x_columns, x_cod, x_pl, 0),
            (x_columns, x_cod, x_pl, 1),
            (k_columns, k_cod, k_pl, 0),
            (k_columns, k_cod, k_pl, 1),
        ]

        def stage2(c, out_ap, m0, width, passes):
            for i in passes:
                columns, cod, pl, half = stage2_operands[i]
                nc.tensor.matmul_mx(
                    out=out_ap,
                    lhsT=columns(cod, c, half).bitcast(FP8X4),
                    lhsT_scale=columns(pl, c, half),
                    rhs=h_cod[:, i, m0 : m0 + width].bitcast(FP8X4),
                    rhs_scale=h_pl[4 * i : P, m0 : m0 + width],
                    start=(i == 0),
                    stop=(i == 3),
                )

        ybank, yb = {}, {}

        def stage2_wide(c):
            ybank[c] = bank("ybank")
            stage2(c, ybank[c][:], 0, 512, range(4))

        def copy_y(c):
            g, t = divmod(c, 4)
            nc.scalar.copy(out=y_sb[g][:, t, :], in_=ybank[c][:])

        def store_y(c):
            g, t = divmod(c, 4)
            nc.sync.dma_start(out=o_v[g][:, t, :], in_=y_sb[g][:, t, :])

        last = {}

        def part_x(c, m0, w):
            last[c, m0] = bank("last")
            stage2(c, last[c, m0][:, :w], m0, w, range(2))

        def part_k(c, m0, w):
            stage2(c, last[c, m0][:, :w], m0, w, range(2, 4))

        def copy_part(c, m0, w):
            nc.scalar.copy(out=y_sb[c // 4][:, c % 4, m0 : m0 + w], in_=last[c, m0][:, :w])

        def copy_part_v(c, m0, w):
            nc.vector.tensor_copy(out=y_sb[c // 4][:, c % 4, m0 : m0 + w], in_=last[c, m0][:, :w])

        def store_part(c, m0, w):
            nc.sync.dma_start(out=o_v[c // 4][:, c % 4, m0 : m0 + w], in_=y_sb[c // 4][:, c % 4, m0 : m0 + w])

        def interleave_y(g, m0, width, engine):
            yb[g, m0] = work.tile([P, 1024], BF16, align_bytes=64, tag="yb", name="yb")
            copy = nc.scalar.copy if engine == "scalar" else nc.vector.tensor_copy
            copy(
                out=yb[g, m0][:, : 4 * width].rearrange("p (m t) -> p m t", t=4),
                in_=y_sb[g][:, :, m0 : m0 + width].rearrange("p t m -> p m t"),
            )

        def quant_y(g, m0, width):
            nc.vector.quantize_mx(
                out=y_cod[g][:, m0 : m0 + width].bitcast(FP8X4),
                scales=y_pl[g][:, m0 : m0 + width],
                in_=yb[g, m0][:, : 4 * width],
            )

        def store_codes(g, m0, width):
            nc.sync.dma_start(
                out=out_1[g].rearrange("p m t -> p (m t)")[:, 4 * m0 : 4 * (m0 + width)].bitcast(I32),
                in_=y_cod[g][:, m0 : m0 + width],
            )

        def store_scales(g):
            for q in range(4):
                eng = nc.sync
                eng.dma_start(
                    out=out_2[g, 4 * q : 4 * q + 4, :].bitcast(I32), in_=y_pl[g][32 * q : 32 * q + 4, :].bitcast(I32)
                )

        def p_of(d, h):
            stage1(d, h, a_cod, 0, pb, "pb")

        def q_of(d, h):
            stage1(d, h, b_cod, 1, qb, "qb")

        def warm_up(count):
            wb = bank("wb")
            for i in range(count):
                nc.tensor.matmul_mx(
                    out=wb[:, 0:P],
                    lhsT=warm_cod[:].bitcast(FP8X4),
                    lhsT_scale=warm_pl[:],
                    rhs=warm_cod[:].bitcast(FP8X4),
                    rhs_scale=warm_pl[:],
                    start=True,
                    stop=True,
                )

        warm_up(8)
        perm_scales(0)
        transpose_x(0)
        copy_x(0)
        transpose_x(1)
        copy_x(1)
        quant_x(0)
        warm_up(8)
        perm(a_cod, a_raw, 0, 2)
        transpose_x(2)
        copy_x(2)
        perm(a_cod, a_raw, 2, 4)
        transpose_x(3)
        copy_x(3)
        quant_x(1)
        warm_up(8)
        perm_scales(1)
        p_of(0, 0)
        copy_p(0, 0)
        perm(b_cod, b_raw, 0, 2)
        p_of(0, 1)
        copy_p(0, 1)
        perm(b_cod, b_raw, 2, 4)
        p_of(1, 0)
        copy_p(1, 0)
        permute_words(0)
        p_of(1, 1)
        copy_p(1, 1)
        q_of(0, 0)
        make_k2(0, 0)
        q_of(0, 1)
        make_k2(0, 1)
        transpose_x(4)
        copy_x(4)
        permute_words(1)
        transpose_x(5)
        copy_x(5)
        make_k3(0)
        q_of(1, 0)
        cast_k2(0)
        quant_x(2)
        q_of(1, 1)
        cast_k2(1)
        make_k2(1, 0)
        transpose_x(6)
        copy_x(6)
        make_k2(1, 1)
        transpose_x(7)
        copy_x(7)
        make_k3(1)
        p_of(2, 0)
        copy_p(2, 0)
        quant_x(3)
        p_of(2, 1)
        copy_p(2, 1)
        quant_k(0)
        q_of(2, 0)
        cast_k2(2)
        make_k2(2, 0)
        q_of(2, 1)
        cast_k2(3)
        make_k2(2, 1)
        p_of(3, 0)
        copy_p(3, 0)
        quant_k(1)
        p_of(3, 1)
        copy_p(3, 1)
        make_k3(2)
        q_of(3, 0)
        cast_k2(4)
        make_k3(3)
        q_of(3, 1)
        cast_k2(5)
        make_k2(3, 0)
        stage2_wide(0)
        copy_y(0)
        make_k2(3, 1)
        store_y(0)
        stage2_wide(1)
        cast_k2(6)
        quant_k(2)
        stage2_wide(2)
        cast_k2(7)
        quant_k(3)
        stage2_wide(3)
        copy_y(1)
        make_k3(4)
        store_y(1)
        copy_y(2)
        make_k3(5)
        store_y(2)
        copy_y(3)
        quant_k(4)
        store_y(3)
        stage2_wide(4)
        copy_y(4)
        make_k3(6)
        store_y(4)
        quant_k(5)
        stage2_wide(5)
        copy_y(5)
        make_k3(7)
        part_x(6, 0, 256)
        quant_k(6)
        part_k(6, 0, 256)
        copy_part(6, 0, 256)
        quant_k(7)
        part_x(7, 0, 256)
        interleave_y(0, 0, 256, "vector")
        part_k(7, 0, 256)
        copy_part(7, 0, 256)
        interleave_y(0, 256, 256, "vector")
        part_x(6, 256, 256)
        quant_y(0, 0, 256)
        part_k(6, 256, 256)
        copy_part(6, 256, 256)
        quant_y(0, 256, 256)
        store_codes(0, 0, 512)
        part_x(7, 256, 128)
        interleave_y(1, 0, 256, "vector")
        store_scales(0)
        part_k(7, 256, 128)
        copy_part(7, 256, 128)
        interleave_y(1, 256, 128, "vector")
        store_y(5)
        part_x(7, 384, 128)
        quant_y(1, 0, 256)
        store_part(6, 0, 512)
        part_k(7, 384, 128)
        copy_part(7, 384, 128)
        interleave_y(1, 384, 128, "vector")
        store_part(7, 0, 512)
        quant_y(1, 256, 128)
        store_codes(1, 0, 256)
        quant_y(1, 384, 128)
        store_codes(1, 256, 256)
        store_scales(1)
